import numpy as np
import ml_dtypes


def mxq(x, axis, fmt="e4m3"):
    dtype, down = {"e4m3": (ml_dtypes.float8_e4m3fn, 7), "e5m2": (ml_dtypes.float8_e5m2, 14)}[fmt]
    v = np.moveaxis(np.asarray(x, np.float32).astype(ml_dtypes.bfloat16).astype(np.float64), axis, -1)
    blocks = v.reshape(v.shape[:-1] + (-1, 32))
    amax = np.abs(blocks).max(-1, keepdims=True)
    byte = np.maximum(np.where(amax > 0, np.frexp(amax)[1] - 1 + 127, 0) - down, 1)
    scale = np.exp2(byte - 127.0)
    codes = (blocks / scale).astype(np.float32).astype(dtype).astype(np.float64)
    return np.moveaxis((codes * scale).reshape(v.shape), -1, axis)


WIDE = False


def mx_kscale(k):
    if not WIDE:
        return np.ones(k)
    levels = np.array([10, -10, 5, -5, 0])
    if k % 512:
        return np.exp2(np.random.permutation(np.resize(levels, k // 32))).repeat(32)
    a = np.empty((k // 512, 16))
    for p in range(k // 512):
        a[p, :8] = np.random.permutation(np.resize(levels, 8))
        for g in range(8):
            far = levels[np.abs(levels - a[p, g]) >= 10]
            a[p, g + 8] = far[np.random.randint(len(far))]
    return np.exp2(a.ravel()).repeat(32)


BF16 = ml_dtypes.bfloat16


def bf(x):
    return np.asarray(x, np.float32).astype(BF16)


def f64(x):
    return np.asarray(x).astype(np.float64)


E2M1 = np.array([0.0, 0.5, 1.0, 1.5, 2.0, 3.0, 4.0, 6.0, -0.0, -0.5, -1.0, -1.5, -2.0, -3.0, -4.0, -6.0])


def pack_weight(w, fmt):
    k, n = w.shape
    w = f64(bf(w)).reshape(k // 32, 32, n)
    amax = np.abs(w).max(1)
    if fmt == "e4m3":
        byte = np.frexp(amax)[1] - 1 + 127 - 7
    else:
        mant, ex = np.frexp(amax / 6.0)
        byte = np.where(mant > 0.5, ex, ex - 1) + 127
    byte = np.clip(np.where(amax > 0, byte, 1), 1, 254)
    scaled = (w * np.exp2(127.0 - byte)[:, None, :]).reshape(k, n).astype(np.float32)
    by_word = np.ascontiguousarray(scaled.reshape(k // 512, 128, 4, n).transpose(0, 1, 3, 2))
    if fmt == "e4m3":
        words = by_word.astype(ml_dtypes.float8_e4m3fn).view(np.uint8)
    else:
        c = by_word.astype(ml_dtypes.float4_e2m1fn).view(np.uint8) & 0xF
        words = c[..., 0::2] | (c[..., 1::2] << 4)
    return np.ascontiguousarray(words), np.ascontiguousarray(byte.astype(np.uint8).reshape(k // 512, 16, n))


def unpack_weight(words, scales, fmt):
    g, p, n, _ = words.shape
    if fmt == "e4m3":
        vals = np.ascontiguousarray(words).view(ml_dtypes.float8_e4m3fn).astype(np.float64)
    else:
        nib = np.empty((g, p, n, 4), np.uint8)
        nib[..., 0::2] = words & 0xF
        nib[..., 1::2] = words >> 4
        vals = E2M1[nib]
    vals = vals * np.repeat(np.exp2(scales.astype(np.float64) - 127.0), 8, axis=1)[..., None]
    return vals.transpose(0, 1, 3, 2).reshape(g * 512, n)
def pack4(w):
    words, scales = pack_weight(w, "e2m1")
    return words.reshape(words.shape[0], 128, -1), scales


def unpack4(words, scales):
    return unpack_weight(words.reshape(words.shape[0], 128, -1, 2), scales, "e2m1")


def planes(Y):
    n, m = Y.shape
    b = f64(bf(Y)).reshape(n // 32, 32, m)
    amax = np.abs(b).max(1)
    byte = np.clip(np.where(amax > 0, np.frexp(amax)[1] - 1 + 127 - 7, 1), 1, 254)
    codes = (b * np.exp2(127.0 - byte)[:, None, :]).reshape(n, m).astype(np.float32).astype(ml_dtypes.float8_e4m3fn).view(np.uint8)
    words = codes.reshape(n // 512, 128, 4, m).transpose(0, 1, 3, 2)
    return np.ascontiguousarray(words), np.ascontiguousarray(byte.astype(np.uint8).reshape(n // 512, 16, m))


P, D, A, N = 1024, 512, 2048, 1536
VOL = 0.6
CASH = 0.7
LEVEL = 0.25


def setup_inputs():
    s = mx_kscale(D)
    t = mx_kscale(A)
    z = np.random.randn(P, D)
    L = VOL * np.random.randn(D, A) / np.sqrt(D)
    median = np.exp(0.3 * np.random.randn(A))
    W = np.random.randn(A, N) / np.sqrt(A)
    cash = CASH + 0.3 * np.random.randn(N)
    guarantee = LEVEL * np.exp(0.3 * np.random.randn(N))
    notional = np.exp(0.7 * np.random.randn(N))
    loadings_words, loadings_scales = pack4(L / s[:, None])
    holdings_words, holdings_scales = pack4(W / t[:, None])
    return {
        "z": bf(z * s[None, :]),
        "loadings_words": loadings_words,
        "loadings_scales": loadings_scales,
        "median": bf(median * t),
        "holdings_words": holdings_words,
        "holdings_scales": holdings_scales,
        "cash": bf(cash),
        "guarantee": bf(guarantee),
        "notional": bf(notional),
    }


def reference(z, loadings_words, loadings_scales, median, holdings_words, holdings_scales, cash, guarantee, notional):
    L = unpack4(loadings_words, loadings_scales)
    X = mxq(f64(z), 1, "e4m3") @ L
    V = f64(median)[None, :] * np.exp(X)
    W = unpack4(holdings_words, holdings_scales)
    B = mxq(V, 1, "e4m3") @ W
    y = f64(notional)[None, :] * np.maximum(B + f64(cash)[None, :], f64(guarantee)[None, :])
    Y = y.T
    words, scales = planes(Y)
    return y, words, scales

@@ -1,0 +1,405 @@
+from contextlib import ExitStack
+
+import concourse.mybir as mybir
+from concourse.masks import make_identity
+
+PATHS, DRIVERS, ASSETS, BASKETS = 1024, 512, 2048, 1536
+FLOPS = 2 * PATHS * DRIVERS * ASSETS + 2 * PATHS * ASSETS * BASKETS
+
+F32 = mybir.dt.float32
+BF16 = mybir.dt.bfloat16
+I32 = mybir.dt.int32
+U32 = mybir.dt.uint32
+U8 = mybir.dt.uint8
+FP8X4 = mybir.dt.float8_e4m3fn_x4
+FP4X4 = mybir.dt.float4_e2m1fn_x4
+ACT = mybir.ActivationFunctionType
+ALU = mybir.AluOpType
+
+P = 128
+LOOKAHEAD = 5
+NATURAL = 2
+
+
+def tile_guaranteed_basket_payoffs_h1_kernel(
+    tc, z, loadings_words, loadings_scales, median, holdings_words, holdings_scales,
+    cash, guarantee, notional, out_0, out_1, out_2,
+):
+    nc = tc.nc
+    with ExitStack() as ctx:
+        keep = ctx.enter_context(tc.tile_pool(name="keep", bufs=1))
+        work = ctx.enter_context(tc.tile_pool(name="work", bufs=2))
+        psum = ctx.enter_context(tc.psum_pool(name="psum", bufs=1))
+        ctx.enter_context(tc.manual_schedule())
+
+        def kept(name, shape, dtype):
+            return keep.tile(shape, dtype, name=name, tag=name, align_bytes=64)
+
+        def passing(name, shape, dtype, bufs):
+            return work.tile(shape, dtype, name=name, tag=name, bufs=bufs, align_bytes=64)
+
+        rings = {"short": [2, 3, 4, 5, 6, 7], "sum": []}
+
+        def bank(kind, shape=None, dtype=F32):
+            number = rings[kind][0]
+            rings[kind] = rings[kind][1:] + [number]
+            return psum.tile(shape or [P, 512], dtype, name="bank%d" % number, tag="bank%d" % number)
+
+        l_scale_raw = kept("l_scale_raw", [P, ASSETS], U8)
+        w_scale_raw = kept("w_scale_raw", [P, 4, BASKETS], U8)
+        warm = kept("warm", [P, 2], F32)
+        nc.vector.memset(l_scale_raw[:].bitcast(I32), 0)
+        nc.vector.memset(warm[:], 0.0)
+        nc.vector.memset(w_scale_raw[:].rearrange("p g n -> p (g n)").bitcast(I32), 0)
+        nc.scalar.activation(out=warm[:, 1:2], in_=warm[:, 0:1], func=ACT.Exp)
+
+        ident = kept("ident", [P, P], F32)
+        make_identity(nc, ident[:])
+        median_sb = kept("median_sb", [P, 4, 4], BF16)
+        nc.gpsimd.dma_start(out=median_sb[:], in_=median.rearrange("(g p t) -> p g t", p=P, t=4))
+        ident_bf = kept("ident_bf", [P, P], BF16)
+        make_identity(nc, ident_bf[:])
+        rows = kept("rows", [P, P], BF16)
+        nc.gpsimd.memset(rows[:], 0.0)
+        slotted = []
+        for i, vec in enumerate((cash, guarantee, notional)):
+            nc.gpsimd.dma_start(out=rows[8 * i:8 * i + 8, :], in_=vec[0:1024].rearrange("(j p) -> j p", p=P))
+        for i, vec in enumerate((cash, guarantee, notional)):
+            one = kept("slotted%d" % i, [P, 4], BF16)
+            nc.gpsimd.dma_start(out=one[:], in_=vec[1024:BASKETS].rearrange("(p t) -> p t", t=4))
+            slotted.append(one)
+
+        z_raw = [kept("z_raw%d" % c, [P, 2, DRIVERS], BF16) for c in range(4)]
+        l_first = kept("l_first", [P, 1024], U8)
+        l_rest = kept("l_rest", [P, 3072], U8)
+        w_raw = [kept("w_raw%d" % b, [P, 4, 1024], U8) for b in range(3)]
+
+        def load_z(c):
+            nc.sync.dma_start(out=z_raw[c][:], in_=z[256 * c:256 * c + 256, :].rearrange("(j p) k -> p j k", p=P))
+
+        def load_w(b):
+            nc.sync.dma_start(
+                out=w_raw[b][:].bitcast(I32),
+                in_=holdings_words[:, :, 1024 * b:1024 * b + 1024].rearrange("g p n -> p g n").bitcast(I32))
+
+        load_z(0)
+        for q in range(4):
+            nc.sync.dma_start(out=l_scale_raw[32 * q:32 * q + 4, :].bitcast(I32),
+                              in_=loadings_scales[0, 4 * q:4 * q + 4, :].bitcast(I32))
+        nc.sync.dma_start(out=l_first[:].bitcast(I32), in_=loadings_words[0, :, 0:1024].bitcast(I32))
+        load_z(1)
+        nc.sync.dma_start(out=l_rest[:].bitcast(I32), in_=loadings_words[0, :, 1024:4096].bitcast(I32))
+        for q in range(4):
+            nc.sync.dma_start(out=w_scale_raw[32 * q:32 * q + 4, :, :].bitcast(I32),
+                              in_=holdings_scales[:, 4 * q:4 * q + 4, :].rearrange("g r n -> r g n").bitcast(I32))
+        load_w(0)
+        load_z(2)
+        load_z(3)
+        load_w(1)
+        load_w(2)
+
+        def copy_on(engine, out, in_):
+            if engine == "scalar":
+                nc.scalar.copy(out=out, in_=in_)
+            else:
+                nc.vector.tensor_copy(out=out, in_=in_)
+
+        def turn_words(sources, grouped, engine):
+            turned = bank("short")
+            for i, source in enumerate(sources):
+                nc.tensor.transpose(turned[:, P * i:P * i + P], source, ident[:])
+            copy_on(engine, grouped.rearrange("p (j r u) -> p j r u", j=2, u=2),
+                    turned[:].rearrange("p (j u r) -> p j r u", j=2, u=2))
+
+        z_grouped, z_codes, z_scales = {}, {}, {}
+
+        def turn_z(c):
+            words = z_raw[c][:].rearrange("p j k -> p (j k)").bitcast(F32)
+            z_grouped[c] = passing("z_grouped", [P, 512], F32, 2)
+            turn_words([words[:, 256 * j + u:256 * j + 256:2] for j in range(2) for u in range(2)],
+                       z_grouped[c][:], "scalar")
+
+        def quantise_z(c):
+            z_codes[c] = kept("z_codes%d" % c, [P, 256], U32)
+            z_scales[c] = kept("z_scales%d" % c, [P, 256], U8)
+            nc.vector.quantize_mx(out=z_codes[c][:].bitcast(FP8X4), scales=z_scales[c][:],
+                                  in_=z_grouped[c][:].bitcast(BF16))
+
+        l_codes, l_scales = {}, {}
+
+        def sort_l(g):
+            raw = l_first[:] if g == 0 else l_rest[:, 1024 * (g - 1):1024 * g]
+            l_codes[g] = kept("l_codes%d" % g, [P, 1024], U8)
+            l_scales[g] = kept("l_scales%d" % g, [P, 512], U8)
+            nc.vector.tensor_copy(out=l_scales[g][:].rearrange("p (t m) -> p t m", t=4),
+                                  in_=l_scale_raw[:, 512 * g:512 * g + 512].rearrange("p (m t) -> p t m", t=4))
+            nc.vector.tensor_copy(out=l_codes[g][:].rearrange("p (t m c) -> p t m c", t=4, c=2),
+                                  in_=raw.rearrange("p (m t c) -> p t m c", t=4, c=2))
+
+        w_codes, w_scales = {}, {}
+
+        def sort_w(b, g):
+            w_codes[b, g] = kept("w_codes%d_%d" % (b, g), [P, 1024], U8)
+            w_scales[b, g] = kept("w_scales%d_%d" % (b, g), [P, 512], U8)
+            nc.vector.tensor_copy(out=w_codes[b, g][:].rearrange("p (t m c) -> p t m c", t=4, c=2),
+                                  in_=w_raw[b][:, g, :].rearrange("p (m t c) -> p t m c", t=4, c=2))
+            nc.vector.tensor_copy(out=w_scales[b, g][:].rearrange("p (t m) -> p t m", t=4),
+                                  in_=w_scale_raw[:, g, 512 * b:512 * b + 512].rearrange("p (m t) -> p t m", t=4))
+
+        growth, prices = {}, {}
+        v_codes = {(h, g): kept("v_codes%d_%d" % (h, g), [P, 512], U32) for h in range(2) for g in range(4)}
+        v_scales = {(h, g): kept("v_scales%d_%d" % (h, g), [P, 512], U8) for h in range(2) for g in range(4)}
+
+        def place(k):
+            return k // 8, (k % 8) // 2, k % 2
+
+        def exponentials(k, pairs=(0, 1)):
+            h, g, q = place(k)
+            c = 2 * h + q
+            if pairs[0] == 0:
+                growth[k] = passing("growth", [P, 2, 256, 2], F32, LOOKAHEAD + 1)
+            for u in pairs:
+                x = bank("short")
+                for e in range(2):
+                    t = 2 * u + e
+                    nc.tensor.matmul_mx(
+                        out=x[:, 256 * e:256 * e + 256],
+                        lhsT=l_codes[g][:, 256 * t:256 * t + 256].bitcast(FP4X4),
+                        lhsT_scale=l_scales[g][:, P * t:P * t + P],
+                        rhs=z_codes[c][:].bitcast(FP8X4), rhs_scale=z_scales[c][:],
+                        start=True, stop=True)
+                nc.scalar.activation(out=growth[k][:, u, :, :], in_=x[:].rearrange("p (e n) -> p n e", e=2),
+                                     func=ACT.Exp)
+
+        def times_median(k):
+            h, g, q = place(k)
+            prices[k] = passing("prices", [P, 1024], BF16, 3)
+            nc.vector.tensor_tensor(
+                out=prices[k][:].rearrange("p (n u e) -> p n u e", u=2, e=2),
+                in0=growth[k][:].rearrange("p u n e -> p n u e"),
+                in1=median_sb[:, g, :].rearrange("p (u e) -> p u e", e=2).unsqueeze(1).to_broadcast([P, 256, 2, 2]),
+                op=ALU.mult)
+
+        def quantise_prices(k):
+            h, g, q = place(k)
+            cols = slice(256 * q, 256 * q + 256)
+            nc.vector.quantize_mx(out=v_codes[h, g][:, cols].bitcast(FP8X4), scales=v_scales[h, g][:, cols],
+                                  in_=prices[k][:])
+
+        natural = kept("natural", [P, 24], BF16)
+
+        def turn_rows():
+            turned = bank("short", [P, P], BF16)
+            nc.tensor.transpose(turned[:], rows[:], ident_bf[:])
+            nc.scalar.copy(out=natural[:], in_=turned[:, 0:24])
+
+        def column(i, b, t):
+            if b < NATURAL:
+                return natural[:, 8 * i + 4 * b + t:8 * i + 4 * b + t + 1]
+            return slotted[i][:, t:t + 1]
+
+        sums, payoff = {}, {}
+
+        def one_pass(b, h, t, g):
+            if g == 0:
+                sums[b, h, t] = bank("sum")
+            if b < NATURAL:
+                codes = w_raw[b][:, g, 256 * t:256 * t + 256]
+                scales = w_scale_raw[:, g, 512 * b + P * t:512 * b + P * t + P]
+            else:
+                codes = w_codes[b, g][:, 256 * t:256 * t + 256]
+                scales = w_scales[b, g][:, P * t:P * t + P]
+            nc.tensor.matmul_mx(out=sums[b, h, t][:], lhsT=codes.bitcast(FP4X4), lhsT_scale=scales,
+                                rhs=v_codes[h, g][:].bitcast(FP8X4), rhs_scale=v_scales[h, g][:],
+                                start=(g == 0), stop=(g == 3))
+
+        def add_cash(b, h, t):
+            if t == 0:
+                payoff[b, h] = passing("payoff", [P, 4, 512], F32, 5)
+            nc.scalar.activation(out=payoff[b, h][:, t, :], in_=sums[b, h, t][:], func=ACT.Identity,
+                                 bias=column(0, b, t))
+
+        def whole_tile(b, h, t):
+            for g in range(4):
+                one_pass(b, h, t, g)
+            add_cash(b, h, t)
+
+        def floor_and_scale(b, h, t):
+            nc.vector.tensor_scalar(out=payoff[b, h][:, t, :], in0=payoff[b, h][:, t, :],
+                                    scalar1=column(1, b, t), scalar2=column(2, b, t), op0=ALU.max, op1=ALU.mult)
+
+        by_path = {}
+
+        def store_paths(b, h, j0, j1):
+            nc.sync.dma_start(
+                out=out_0[512 * h + P * j0:512 * h + P * j1, 512 * b:512 * b + 512].rearrange("(j p) n -> p j n", p=P),
+                in_=by_path[b, h][:, j0:j1, :])
+
+        def turn_payoff(b, h, engines, first=0, singly=False):
+            if first == 0:
+                by_path[b, h] = passing("by_path", [P, 4, 512], F32, 3)
+            blocks = range(first, first + len(engines))
+            turned = {j: bank("short") for j in blocks}
+            for t in range(4):
+                for j in blocks:
+                    nc.tensor.transpose(turned[j][:, P * t:P * t + P], payoff[b, h][:, t, P * j:P * j + P], ident[:])
+            for j in blocks:
+                if b < NATURAL:
+                    copy_on(engines[j - first], by_path[b, h][:, j, :], turned[j][:])
+                else:
+                    copy_on(engines[j - first], by_path[b, h][:, j, :].rearrange("p (m t) -> p m t", t=4),
+                            turned[j][:].rearrange("p (t m) -> p m t", t=4))
+                if singly:
+                    store_paths(b, h, j, j + 1)
+            if not singly:
+                store_paths(b, h, first, first + len(engines))
+
+        y_grouped, y_sorted = {}, {}
+        y_scales = [kept("y_scales%d" % b, [P, PATHS], U8) for b in range(3)]
+
+        def round_payoff(b, h):
+            if b < NATURAL:
+                y_sorted[b, h] = passing("y_sorted", [P, 2048], BF16, 2)
+                nc.vector.tensor_copy(
+                    out=y_sorted[b, h][:].rearrange("p (j u m e) -> p j u m e", j=4, u=2, e=2),
+                    in_=by_path[b, h][:].rearrange("p j (m u e) -> p j u m e", u=2, e=2))
+            else:
+                y_grouped[b, h] = passing("y_grouped", [P, 1024], F32, 2)
+                nc.vector.tensor_copy(
+                    out=y_grouped[b, h][:].bitcast(BF16).rearrange("p (c i t) -> p c t i", i=2, t=4),
+                    in_=payoff[b, h][:].rearrange("p t (c i) -> p c t i", i=2))
+
+        def turn_rounded(b, h, engine="scalar"):
+            words = y_sorted[b, h][:].bitcast(F32)
+            y_grouped[b, h] = passing("y_grouped", [P, 1024], F32, 2)
+            for half in range(2):
+                turn_words([words[:, 512 * half + P * i:512 * half + P * i + P] for i in range(4)],
+                           y_grouped[b, h][:, 512 * half:512 * half + 512], engine)
+
+        def quantise_payoff(b, h):
+            codes = passing("y_codes", [P, 512], U32, 2)
+            cols = slice(512 * h, 512 * h + 512)
+            nc.vector.quantize_mx(out=codes[:].bitcast(FP8X4), scales=y_scales[b][:, cols],
+                                  in_=y_grouped[b, h][:].bitcast(BF16))
+            nc.sync.dma_start(out=out_1[b, :, cols, :].rearrange("p m t -> p (m t)").bitcast(I32),
+                              in_=codes[:].bitcast(I32))
+            if h == 1:
+                for q in range(4):
+                    nc.sync.dma_start(out=out_2[b, 4 * q:4 * q + 4, :].bitcast(I32),
+                                      in_=y_scales[b][32 * q:32 * q + 4, :].bitcast(I32))
+
+        S, V = "scalar", "vector"
+        open_tiles = [(0, 0), (0, 1), (0, 2), (0, 3), (1, 0)]
+        waiting = []
+
+        def issue(count):
+            for i in range(min(count, len(waiting))):
+                b, h, t, g = waiting[0]
+                waiting.remove(waiting[0])
+                one_pass(b, h, t, g)
+                if g == 3:
+                    add_cash(b, h, t)
+
+        def floors(b, h):
+            for t in range(4):
+                floor_and_scale(b, h, t)
+
+        turn_z(0)
+        sort_l(0)
+        quantise_z(0)
+        turn_z(1)
+        exponentials(0)
+        quantise_z(1)
+        exponentials(1)
+        sort_l(1)
+        turn_rows()
+        exponentials(2)
+        times_median(0)
+        exponentials(3)
+        times_median(1)
+        turn_z(2)
+        turn_z(3)
+        quantise_prices(0)
+        sort_l(2)
+        quantise_prices(1)
+        exponentials(4)
+        sort_l(3)
+        exponentials(5)
+        rings["short"], rings["sum"] = [0, 1, 2], [3, 4, 5, 6, 7]
+        ready = [(b, 0, t, 0) for b, t in open_tiles]
+        for k in range(2, 17):
+            ahead = k + LOOKAHEAD - 1
+            if k < 16:
+                times_median(k)
+            if k in (2, 3):
+                quantise_z(k)
+            if k == 16:
+                sort_w(2, 0)
+            if k > 2:
+                quantise_prices(k - 1)
+            if k == 11:
+                floors(0, 0)
+            if k == 13:
+                floors(1, 0)
+            waiting.extend(ready)
+            ready = []
+            per = 2 if k < 9 else 3
+            for u in range(2):
+                if ahead < 16:
+                    exponentials(ahead, (u,))
+                issue(per)
+            h, g, q = place(k - 1)
+            if q == 1 and k > 2:
+                ready = [(b, h, t, g) for b, t in open_tiles]
+                if g == 3:
+                    ready = ready + [(1, h, t, g2) for t in range(1, 4) for g2 in range(4)]
+            if k == 12:
+                turn_payoff(0, 0, [S, S])
+            if k == 13:
+                turn_payoff(0, 0, [S, S], first=2)
+            if k == 14:
+                turn_payoff(1, 0, [S, S])
+            if k == 15:
+                turn_payoff(1, 0, [S, S], first=2)
+        waiting.extend(ready)
+        for g in range(1, 4):
+            sort_w(2, g)
+        round_payoff(0, 0)
+        issue(9)
+        rings["short"], rings["sum"] = [0, 1, 2, 3], [4, 5, 6, 7]
+        issue(8)
+        floors(0, 1)
+        turn_rounded(0, 0)
+        whole_tile(2, 0, 0)
+        round_payoff(1, 0)
+        turn_payoff(0, 1, [S, S, S, V])
+        floors(1, 1)
+        quantise_payoff(0, 0)
+        whole_tile(2, 0, 1)
+        turn_rounded(1, 0)
+        whole_tile(2, 0, 2)
+        round_payoff(0, 1)
+        turn_payoff(1, 1, [S, S, S, V])
+        quantise_payoff(1, 0)
+        whole_tile(2, 0, 3)
+        turn_rounded(0, 1)
+        whole_tile(2, 1, 0)
+        round_payoff(1, 1)
+        floors(2, 0)
+        quantise_payoff(0, 1)
+        whole_tile(2, 1, 1)
+        turn_rounded(1, 1)
+        turn_payoff(2, 0, [S, S])
+        whole_tile(2, 1, 2)
+        round_payoff(2, 0)
+        floor_and_scale(2, 1, 0)
+        floor_and_scale(2, 1, 1)
+        quantise_payoff(1, 1)
+        turn_payoff(2, 0, [S, S], first=2)
+        whole_tile(2, 1, 3)
+        floor_and_scale(2, 1, 2)
+        quantise_payoff(2, 0)
+        floor_and_scale(2, 1, 3)
+        round_payoff(2, 1)
+        turn_payoff(2, 1, [S, S, S, S], singly=True)
+        quantise_payoff(2, 1)

@@ -1,4 +1,5 @@
 from contextlib import ExitStack
+from functools import partial
 
 import concourse.mybir as mybir
 from concourse.masks import make_identity
@@ -18,7 +19,7 @@ ALU = mybir.AluOpType
 
 P = 128
 LOOKAHEAD = 5
-NATURAL = 2
+NATURAL = ((0, 0), (1, 0), (0, 1))
 
 
 def tile_guaranteed_basket_payoffs_h1_kernel(
@@ -51,23 +52,17 @@ def tile_guaranteed_basket_payoffs_h1_kernel(
         nc.vector.memset(l_scale_raw[:].bitcast(I32), 0)
         nc.vector.memset(warm[:], 0.0)
         nc.vector.memset(w_scale_raw[:].rearrange("p g n -> p (g n)").bitcast(I32), 0)
+        median_sb = kept("median_sb", [P, 4, 4], BF16)
+        nc.scalar.dma_start(out=median_sb[:], in_=median.rearrange("(g p t) -> p g t", p=P, t=4))
         nc.scalar.activation(out=warm[:, 1:2], in_=warm[:, 0:1], func=ACT.Exp)
 
         ident = kept("ident", [P, P], F32)
         make_identity(nc, ident[:])
-        median_sb = kept("median_sb", [P, 4, 4], BF16)
-        nc.gpsimd.dma_start(out=median_sb[:], in_=median.rearrange("(g p t) -> p g t", p=P, t=4))
-        ident_bf = kept("ident_bf", [P, P], BF16)
-        make_identity(nc, ident_bf[:])
         rows = kept("rows", [P, P], BF16)
         nc.gpsimd.memset(rows[:], 0.0)
-        slotted = []
-        for i, vec in enumerate((cash, guarantee, notional)):
-            nc.gpsimd.dma_start(out=rows[8 * i:8 * i + 8, :], in_=vec[0:1024].rearrange("(j p) -> j p", p=P))
-        for i, vec in enumerate((cash, guarantee, notional)):
-            one = kept("slotted%d" % i, [P, 4], BF16)
-            nc.gpsimd.dma_start(out=one[:], in_=vec[1024:BASKETS].rearrange("(p t) -> p t", t=4))
-            slotted.append(one)
+        ident_bf = kept("ident_bf", [P, P], BF16)
+        make_identity(nc, ident_bf[:])
+        slotted = [kept("slotted%d" % i, [P, 3, 4], BF16) for i in range(3)]
 
         z_raw = [kept("z_raw%d" % c, [P, 2, DRIVERS], BF16) for c in range(4)]
         l_first = kept("l_first", [P, 1024], U8)
@@ -92,11 +87,15 @@ def tile_guaranteed_basket_payoffs_h1_kernel(
         for q in range(4):
             nc.sync.dma_start(out=w_scale_raw[32 * q:32 * q + 4, :, :].bitcast(I32),
                               in_=holdings_scales[:, 4 * q:4 * q + 4, :].rearrange("g r n -> r g n").bitcast(I32))
-        load_w(0)
         load_z(2)
         load_z(3)
+        for i, vec in enumerate((cash, guarantee, notional)):
+            nc.sync.dma_start(out=rows[16 * i:16 * i + 12, :], in_=vec.rearrange("(j p) -> j p", p=P))
+        load_w(0)
         load_w(1)
         load_w(2)
+        for i, vec in enumerate((cash, guarantee, notional)):
+            nc.sync.dma_start(out=slotted[i][:], in_=vec.rearrange("(b p t) -> p b t", p=P, t=4))
 
         def copy_on(engine, out, in_):
             if engine == "scalar":
@@ -104,20 +103,20 @@ def tile_guaranteed_basket_payoffs_h1_kernel(
             else:
                 nc.vector.tensor_copy(out=out, in_=in_)
 
-        def turn_words(sources, grouped, engine):
+        def turn_words(sources, grouped):
             turned = bank("short")
             for i, source in enumerate(sources):
                 nc.tensor.transpose(turned[:, P * i:P * i + P], source, ident[:])
-            copy_on(engine, grouped.rearrange("p (j r u) -> p j r u", j=2, u=2),
-                    turned[:].rearrange("p (j u r) -> p j r u", j=2, u=2))
+            return lambda engine: copy_on(engine, grouped.rearrange("p (j r u) -> p j r u", j=2, u=2),
+                                          turned[:].rearrange("p (j u r) -> p j r u", j=2, u=2))
 
         z_grouped, z_codes, z_scales = {}, {}, {}
 
         def turn_z(c):
             words = z_raw[c][:].rearrange("p j k -> p (j k)").bitcast(F32)
             z_grouped[c] = passing("z_grouped", [P, 512], F32, 2)
-            turn_words([words[:, 256 * j + u:256 * j + 256:2] for j in range(2) for u in range(2)],
-                       z_grouped[c][:], "scalar")
+            return turn_words([words[:, 256 * j + u:256 * j + 256:2] for j in range(2) for u in range(2)],
+                              z_grouped[c][:])
 
         def quantise_z(c):
             z_codes[c] = kept("z_codes%d" % c, [P, 256], U32)
@@ -186,24 +185,24 @@ def tile_guaranteed_basket_payoffs_h1_kernel(
             nc.vector.quantize_mx(out=v_codes[h, g][:, cols].bitcast(FP8X4), scales=v_scales[h, g][:, cols],
                                   in_=prices[k][:])
 
-        natural = kept("natural", [P, 24], BF16)
+        natural = kept("natural", [P, 48], BF16)
 
         def turn_rows():
             turned = bank("short", [P, P], BF16)
             nc.tensor.transpose(turned[:], rows[:], ident_bf[:])
-            nc.scalar.copy(out=natural[:], in_=turned[:, 0:24])
+            nc.scalar.copy(out=natural[:], in_=turned[:, 0:48])
 
-        def column(i, b, t):
-            if b < NATURAL:
-                return natural[:, 8 * i + 4 * b + t:8 * i + 4 * b + t + 1]
-            return slotted[i][:, t:t + 1]
+        def column(i, b, h, t):
+            if (b, h) in NATURAL:
+                return natural[:, 16 * i + 4 * b + t:16 * i + 4 * b + t + 1]
+            return slotted[i][:, b, t:t + 1]
 
-        sums, payoff = {}, {}
+        sums, payoff, pair, regrouped = {}, {}, [], {}
 
         def one_pass(b, h, t, g):
             if g == 0:
                 sums[b, h, t] = bank("sum")
-            if b < NATURAL:
+            if (b, h) in NATURAL:
                 codes = w_raw[b][:, g, 256 * t:256 * t + 256]
                 scales = w_scale_raw[:, g, 512 * b + P * t:512 * b + P * t + P]
             else:
@@ -214,10 +213,14 @@ def tile_guaranteed_basket_payoffs_h1_kernel(
                                 start=(g == 0), stop=(g == 3))
 
         def add_cash(b, h, t):
-            if t == 0:
-                payoff[b, h] = passing("payoff", [P, 4, 512], F32, 5)
+            if (b, h) == (0, 0) and t == 0:
+                both = kept("both", [P, 4, 2, 512], F32)
+                pair.append(both)
+                payoff[0, 0], payoff[1, 0] = both[:, :, 0, :], both[:, :, 1, :]
+            elif t == 0 and (b, h) != (1, 0):
+                payoff[b, h] = passing("payoff", [P, 4, 512], F32, 5)[:]
             nc.scalar.activation(out=payoff[b, h][:, t, :], in_=sums[b, h, t][:], func=ACT.Identity,
-                                 bias=column(0, b, t))
+                                 bias=column(0, b, h, t))
 
         def whole_tile(b, h, t):
             for g in range(4):
@@ -226,7 +229,7 @@ def tile_guaranteed_basket_payoffs_h1_kernel(
 
         def floor_and_scale(b, h, t):
             nc.vector.tensor_scalar(out=payoff[b, h][:, t, :], in0=payoff[b, h][:, t, :],
-                                    scalar1=column(1, b, t), scalar2=column(2, b, t), op0=ALU.max, op1=ALU.mult)
+                                    scalar1=column(1, b, h, t), scalar2=column(2, b, h, t), op0=ALU.max, op1=ALU.mult)
 
         by_path = {}
 
@@ -235,61 +238,65 @@ def tile_guaranteed_basket_payoffs_h1_kernel(
                 out=out_0[512 * h + P * j0:512 * h + P * j1, 512 * b:512 * b + 512].rearrange("(j p) n -> p j n", p=P),
                 in_=by_path[b, h][:, j0:j1, :])
 
-        def turn_payoff(b, h, engines, first=0, singly=False):
-            if first == 0:
+        def empty_block(b, h, j, turned, engine, stored):
+            if (b, h) in NATURAL:
+                copy_on(engine, by_path[b, h][:, j, :], turned[:])
+            else:
+                copy_on(engine, by_path[b, h][:, j, :].rearrange("p (m t) -> p m t", t=4),
+                        turned[:].rearrange("p (t m) -> p m t", t=4))
+            if (j + 1) % stored == 0:
+                store_paths(b, h, j + 1 - stored, j + 1)
+
+        def turn_payoff(b, h, stored=2, blocks=(0, 1, 2, 3)):
+            if blocks[0] == 0:
                 by_path[b, h] = passing("by_path", [P, 4, 512], F32, 3)
-            blocks = range(first, first + len(engines))
             turned = {j: bank("short") for j in blocks}
             for t in range(4):
                 for j in blocks:
                     nc.tensor.transpose(turned[j][:, P * t:P * t + P], payoff[b, h][:, t, P * j:P * j + P], ident[:])
-            for j in blocks:
-                if b < NATURAL:
-                    copy_on(engines[j - first], by_path[b, h][:, j, :], turned[j][:])
-                else:
-                    copy_on(engines[j - first], by_path[b, h][:, j, :].rearrange("p (m t) -> p m t", t=4),
-                            turned[j][:].rearrange("p (t m) -> p m t", t=4))
-                if singly:
-                    store_paths(b, h, j, j + 1)
-            if not singly:
-                store_paths(b, h, first, first + len(engines))
+            return [partial(empty_block, b, h, j, turned[j], stored=stored) for j in blocks]
 
         y_grouped, y_sorted = {}, {}
-        y_scales = [kept("y_scales%d" % b, [P, PATHS], U8) for b in range(3)]
+        y_scales = [kept("y_scales%d" % h, [P, 3, 512], U8) for h in range(2)]
 
-        def round_payoff(b, h):
-            if b < NATURAL:
-                y_sorted[b, h] = passing("y_sorted", [P, 2048], BF16, 2)
-                nc.vector.tensor_copy(
-                    out=y_sorted[b, h][:].rearrange("p (j u m e) -> p j u m e", j=4, u=2, e=2),
-                    in_=by_path[b, h][:].rearrange("p j (m u e) -> p j u m e", u=2, e=2))
+        def regroup(b, h):
+            if (b, h) == (0, 0):
+                source = pair[0][:]
+                target = kept("regrouped", [P, 4, 2, 512], F32)[:]
+                regrouped[0, 0], regrouped[1, 0] = target[:, :, 0, :], target[:, :, 1, :]
             else:
-                y_grouped[b, h] = passing("y_grouped", [P, 1024], F32, 2)
-                nc.vector.tensor_copy(
-                    out=y_grouped[b, h][:].bitcast(BF16).rearrange("p (c i t) -> p c t i", i=2, t=4),
-                    in_=payoff[b, h][:].rearrange("p t (c i) -> p c t i", i=2))
+                source = payoff[b, h].unsqueeze(2)
+                regrouped[b, h] = passing("payoff", [P, 4, 512], F32, 5)[:]
+                target = regrouped[b, h].unsqueeze(2)
+            for j in range(4):
+                for t in range(4):
+                    nc.sync.dma_start(out=target[32 * j:32 * j + 32, t, :, :], in_=source[t:P:4, j, :, :])
 
-        def turn_rounded(b, h, engine="scalar"):
-            words = y_sorted[b, h][:].bitcast(F32)
-            y_grouped[b, h] = passing("y_grouped", [P, 1024], F32, 2)
-            for half in range(2):
-                turn_words([words[:, 512 * half + P * i:512 * half + P * i + P] for i in range(4)],
-                           y_grouped[b, h][:, 512 * half:512 * half + 512], engine)
+        def round_payoff(b, h, engine="vector", width=512, starts=(0,)):
+            source = regrouped[b, h] if (b, h) in NATURAL else payoff[b, h]
+            if starts[0] == 0:
+                y_grouped[b, h] = passing("y_grouped", [P, 2048], BF16, 3)
+            for a in starts:
+                copy_on(engine,
+                        y_grouped[b, h][:, 4 * a:4 * a + 4 * width].rearrange("p (c i t) -> p c t i", i=2, t=4),
+                        source[:, :, a:a + width].rearrange("p t (c i) -> p c t i", i=2))
 
         def quantise_payoff(b, h):
-            codes = passing("y_codes", [P, 512], U32, 2)
+            codes = passing("y_codes", [P, 512], U32, 3)
             cols = slice(512 * h, 512 * h + 512)
-            nc.vector.quantize_mx(out=codes[:].bitcast(FP8X4), scales=y_scales[b][:, cols],
-                                  in_=y_grouped[b, h][:].bitcast(BF16))
+            nc.vector.quantize_mx(out=codes[:].bitcast(FP8X4), scales=y_scales[h][:, b, :],
+                                  in_=y_grouped[b, h][:])
             nc.sync.dma_start(out=out_1[b, :, cols, :].rearrange("p m t -> p (m t)").bitcast(I32),
                               in_=codes[:].bitcast(I32))
-            if h == 1:
-                for q in range(4):
-                    nc.sync.dma_start(out=out_2[b, 4 * q:4 * q + 4, :].bitcast(I32),
-                                      in_=y_scales[b][32 * q:32 * q + 4, :].bitcast(I32))
+
+        def store_scales(h):
+            for q in range(4):
+                nc.sync.dma_start(
+                    out=out_2[:, 4 * q:4 * q + 4, 512 * h:512 * h + 512].rearrange("b r m -> r b m").bitcast(I32),
+                    in_=y_scales[h][32 * q:32 * q + 4, :, :].bitcast(I32))
 
         S, V = "scalar", "vector"
-        open_tiles = [(0, 0), (0, 1), (0, 2), (0, 3), (1, 0)]
+        open_tiles = {0: [(0, 0), (0, 1), (0, 2), (0, 3), (1, 0)], 1: [(0, 0), (0, 1), (0, 2), (0, 3)]}
         waiting = []
 
         def issue(count):
@@ -304,102 +311,142 @@ def tile_guaranteed_basket_payoffs_h1_kernel(
             for t in range(4):
                 floor_and_scale(b, h, t)
 
-        turn_z(0)
+        def passes(h, g):
+            waiting.extend([(b, h, t, g) for b, t in open_tiles[h]])
+
+        turn_z(0)(S)
         sort_l(0)
         quantise_z(0)
-        turn_z(1)
+        turn_z(1)(S)
         exponentials(0)
+        sort_l(1)
         quantise_z(1)
         exponentials(1)
-        sort_l(1)
-        turn_rows()
+        sort_l(2)
         exponentials(2)
         times_median(0)
         exponentials(3)
         times_median(1)
-        turn_z(2)
-        turn_z(3)
         quantise_prices(0)
-        sort_l(2)
-        quantise_prices(1)
-        exponentials(4)
         sort_l(3)
+        quantise_prices(1)
+        empty = [turn_z(2), turn_z(3)]
+        turn_rows()
+        exponentials(4)
+        empty[0](S)
         exponentials(5)
+        empty[1](S)
         rings["short"], rings["sum"] = [0, 1, 2], [3, 4, 5, 6, 7]
-        ready = [(b, 0, t, 0) for b, t in open_tiles]
-        for k in range(2, 17):
-            ahead = k + LOOKAHEAD - 1
-            if k < 16:
-                times_median(k)
-            if k in (2, 3):
-                quantise_z(k)
-            if k == 16:
-                sort_w(2, 0)
+        passes(0, 0)
+        for k in range(2, 8):
+            times_median(k)
             if k > 2:
                 quantise_prices(k - 1)
-            if k == 11:
-                floors(0, 0)
-            if k == 13:
-                floors(1, 0)
-            waiting.extend(ready)
-            ready = []
-            per = 2 if k < 9 else 3
+            if k in (2, 3):
+                quantise_z(k)
             for u in range(2):
-                if ahead < 16:
-                    exponentials(ahead, (u,))
-                issue(per)
-            h, g, q = place(k - 1)
-            if q == 1 and k > 2:
-                ready = [(b, h, t, g) for b, t in open_tiles]
-                if g == 3:
-                    ready = ready + [(1, h, t, g2) for t in range(1, 4) for g2 in range(4)]
-            if k == 12:
-                turn_payoff(0, 0, [S, S])
-            if k == 13:
-                turn_payoff(0, 0, [S, S], first=2)
-            if k == 14:
-                turn_payoff(1, 0, [S, S])
-            if k == 15:
-                turn_payoff(1, 0, [S, S], first=2)
-        waiting.extend(ready)
+                exponentials(k + 4, (u,))
+                issue(2)
+            if k in (4, 6):
+                passes(0, k // 2 - 1)
+        sort_w(2, 0)
+        quantise_prices(7)
+        passes(0, 3)
+        issue(6)
         for g in range(1, 4):
             sort_w(2, g)
-        round_payoff(0, 0)
-        issue(9)
-        rings["short"], rings["sum"] = [0, 1, 2, 3], [4, 5, 6, 7]
-        issue(8)
-        floors(0, 1)
-        turn_rounded(0, 0)
+        rings["short"], rings["sum"] = [0, 1, 2, 6, 7], [3, 4, 5]
+        whole_tile(1, 0, 1)
+        floors(0, 0)
+        whole_tile(1, 0, 2)
+        times_median(8)
+        exponentials(12)
+        whole_tile(1, 0, 3)
+        times_median(9)
+        quantise_prices(8)
+        for step in turn_payoff(0, 0):
+            step(S)
         whole_tile(2, 0, 0)
-        round_payoff(1, 0)
-        turn_payoff(0, 1, [S, S, S, V])
-        floors(1, 1)
-        quantise_payoff(0, 0)
+        floors(1, 0)
+        regroup(0, 0)
+        quantise_prices(9)
+        exponentials(13)
         whole_tile(2, 0, 1)
-        turn_rounded(1, 0)
+        times_median(10)
+        exponentials(14)
         whole_tile(2, 0, 2)
-        round_payoff(0, 1)
-        turn_payoff(1, 1, [S, S, S, V])
-        quantise_payoff(1, 0)
+        times_median(11)
+        quantise_prices(10)
+        for step in turn_payoff(1, 0):
+            step(S)
         whole_tile(2, 0, 3)
-        turn_rounded(0, 1)
-        whole_tile(2, 1, 0)
-        round_payoff(1, 1)
+        quantise_prices(11)
+        exponentials(15)
+        times_median(12)
+        rings["short"], rings["sum"] = [1, 2, 7, 0], [4, 5, 6, 3]
+        passes(1, 0)
+        issue(4)
+        times_median(13)
+        quantise_prices(12)
+        times_median(14)
+        quantise_prices(13)
         floors(2, 0)
-        quantise_payoff(0, 1)
+        passes(1, 1)
+        issue(4)
+        round_payoff(2, 0, S, 128, (0, 128))
+        sort_w(1, 0)
+        times_median(15)
+        quantise_prices(14)
+        sort_w(1, 1)
+        quantise_prices(15)
+        for step in turn_payoff(2, 0):
+            step(S)
+        passes(1, 2)
+        issue(4)
+        passes(1, 3)
+        issue(4)
+        rings["short"], rings["sum"] = [7, 0, 1, 2, 3], [4, 5, 6]
+        sort_w(1, 2)
+        round_payoff(0, 0)
+        floors(0, 1)
+        regroup(0, 1)
+        quantise_payoff(0, 0)
+        whole_tile(2, 1, 0)
         whole_tile(2, 1, 1)
-        turn_rounded(1, 1)
-        turn_payoff(2, 0, [S, S])
-        whole_tile(2, 1, 2)
-        round_payoff(2, 0)
+        round_payoff(2, 0, S, 128, (256,))
+        sort_w(1, 3)
+        round_payoff(1, 0)
+        for step in turn_payoff(0, 1):
+            step(S)
         floor_and_scale(2, 1, 0)
         floor_and_scale(2, 1, 1)
-        quantise_payoff(1, 1)
-        turn_payoff(2, 0, [S, S], first=2)
+        quantise_payoff(1, 0)
+        whole_tile(2, 1, 2)
         whole_tile(2, 1, 3)
+        round_payoff(2, 0, S, 128, (384,))
         floor_and_scale(2, 1, 2)
-        quantise_payoff(2, 0)
         floor_and_scale(2, 1, 3)
+        whole_tile(1, 1, 0)
+        quantise_payoff(2, 0)
+        store_scales(0)
         round_payoff(2, 1)
-        turn_payoff(2, 1, [S, S, S, S], singly=True)
+        for step in turn_payoff(2, 1):
+            step(S)
+        floor_and_scale(1, 1, 0)
         quantise_payoff(2, 1)
+        whole_tile(1, 1, 1)
+        round_payoff(0, 1)
+        whole_tile(1, 1, 2)
+        floor_and_scale(1, 1, 1)
+        quantise_payoff(0, 1)
+        floor_and_scale(1, 1, 2)
+        whole_tile(1, 1, 3)
+        floor_and_scale(1, 1, 3)
+        round_payoff(1, 1)
+        last = turn_payoff(1, 1, stored=1)
+        last[0](S)
+        last[1](S)
+        quantise_payoff(1, 1)
+        last[2](S)
+        last[3](V)
+        store_scales(1)

@@ -47,7 +47,7 @@ def tile_guaranteed_basket_payoffs_h1_kernel(
             return psum.tile(shape or [P, 512], dtype, name="bank%d" % number, tag="bank%d" % number)
 
         l_scale_raw = kept("l_scale_raw", [P, ASSETS], U8)
-        w_scale_raw = kept("w_scale_raw", [P, 4, BASKETS], U8)
+        w_scale_raw = kept("w_scale_raw", [P, 4, 1024], U8)
         warm = kept("warm", [P, 2], F32)
         nc.vector.memset(l_scale_raw[:].bitcast(I32), 0)
         nc.vector.memset(warm[:], 0.0)
@@ -62,6 +62,10 @@ def tile_guaranteed_basket_payoffs_h1_kernel(
         nc.gpsimd.memset(rows[:], 0.0)
         ident_bf = kept("ident_bf", [P, P], BF16)
         make_identity(nc, ident_bf[:])
+        w_scales = {b: kept("w_scales%d" % b, [P, 4, 512], U8) for b in (1, 2)}
+        for b in (2, 1):
+            nc.gpsimd.memset(w_scales[b][:].rearrange("p g n -> p (g n)").bitcast(I32), 0)
+        packed = kept("packed", [P, 1, 512], U8)
         slotted = [kept("slotted%d" % i, [P, 3, 4], BF16) for i in range(3)]
 
         z_raw = [kept("z_raw%d" % c, [P, 2, DRIVERS], BF16) for c in range(4)]
@@ -86,12 +90,16 @@ def tile_guaranteed_basket_payoffs_h1_kernel(
         nc.sync.dma_start(out=l_rest[:].bitcast(I32), in_=loadings_words[0, :, 1024:4096].bitcast(I32))
         for q in range(4):
             nc.sync.dma_start(out=w_scale_raw[32 * q:32 * q + 4, :, :].bitcast(I32),
-                              in_=holdings_scales[:, 4 * q:4 * q + 4, :].rearrange("g r n -> r g n").bitcast(I32))
+                              in_=holdings_scales[:, 4 * q:4 * q + 4, 0:1024].rearrange("g r n -> r g n").bitcast(I32))
         load_z(2)
         load_z(3)
         for i, vec in enumerate((cash, guarantee, notional)):
             nc.sync.dma_start(out=rows[16 * i:16 * i + 12, :], in_=vec.rearrange("(j p) -> j p", p=P))
         load_w(0)
+        for b in (1, 2):
+            nc.sync.dma_start(
+                out=packed[64 * (b - 1):64 * b, 0, :].bitcast(I32),
+                in_=holdings_scales[:, :, 512 * b:512 * b + 512].rearrange("g q n -> (g q) n").bitcast(I32))
         load_w(1)
         load_w(2)
         for i, vec in enumerate((cash, guarantee, notional)):
@@ -110,40 +118,53 @@ def tile_guaranteed_basket_payoffs_h1_kernel(
             return lambda engine: copy_on(engine, grouped.rearrange("p (j r u) -> p j r u", j=2, u=2),
                                           turned[:].rearrange("p (j u r) -> p j r u", j=2, u=2))
 
-        z_grouped, z_codes, z_scales = {}, {}, {}
+        z_grouped = [kept("z_grouped%d" % h, [P, 1024], F32) for h in range(2)]
+        z_codes = [kept("z_codes%d" % h, [P, 512], U32) for h in range(2)]
+        z_scales = [kept("z_scales%d" % h, [P, 512], U8) for h in range(2)]
 
         def turn_z(c):
             words = z_raw[c][:].rearrange("p j k -> p (j k)").bitcast(F32)
-            z_grouped[c] = passing("z_grouped", [P, 512], F32, 2)
             return turn_words([words[:, 256 * j + u:256 * j + 256:2] for j in range(2) for u in range(2)],
-                              z_grouped[c][:])
+                              z_grouped[c // 2][:, 512 * (c % 2):512 * (c % 2) + 512])
 
-        def quantise_z(c):
-            z_codes[c] = kept("z_codes%d" % c, [P, 256], U32)
-            z_scales[c] = kept("z_scales%d" % c, [P, 256], U8)
-            nc.vector.quantize_mx(out=z_codes[c][:].bitcast(FP8X4), scales=z_scales[c][:],
-                                  in_=z_grouped[c][:].bitcast(BF16))
+        def quantise_z(h, first, last):
+            nc.vector.quantize_mx(out=z_codes[h][:, first:last].bitcast(FP8X4), scales=z_scales[h][:, first:last],
+                                  in_=z_grouped[h][:, 2 * first:2 * last].bitcast(BF16))
 
-        l_codes, l_scales = {}, {}
+        def sort_codes(target, raw):
+            nc.vector.tensor_copy(out=target.rearrange("p g (t m c) -> p g t m c", t=4, c=2),
+                                  in_=raw.rearrange("p g (m t c) -> p g t m c", t=4, c=2))
 
-        def sort_l(g):
-            raw = l_first[:] if g == 0 else l_rest[:, 1024 * (g - 1):1024 * g]
-            l_codes[g] = kept("l_codes%d" % g, [P, 1024], U8)
-            l_scales[g] = kept("l_scales%d" % g, [P, 512], U8)
-            nc.vector.tensor_copy(out=l_scales[g][:].rearrange("p (t m) -> p t m", t=4),
-                                  in_=l_scale_raw[:, 512 * g:512 * g + 512].rearrange("p (m t) -> p t m", t=4))
-            nc.vector.tensor_copy(out=l_codes[g][:].rearrange("p (t m c) -> p t m c", t=4, c=2),
-                                  in_=raw.rearrange("p (m t c) -> p t m c", t=4, c=2))
+        def sort_scales(target, raw):
+            nc.vector.tensor_copy(out=target.rearrange("p g (t m) -> p g t m", t=4),
+                                  in_=raw.rearrange("p g (m t) -> p g t m", t=4))
 
-        w_codes, w_scales = {}, {}
+        l_codes = kept("l_codes", [P, 4, 1024], U8)
+        l_scales = kept("l_scales", [P, 4, 512], U8)
 
-        def sort_w(b, g):
-            w_codes[b, g] = kept("w_codes%d_%d" % (b, g), [P, 1024], U8)
-            w_scales[b, g] = kept("w_scales%d_%d" % (b, g), [P, 512], U8)
-            nc.vector.tensor_copy(out=w_codes[b, g][:].rearrange("p (t m c) -> p t m c", t=4, c=2),
-                                  in_=w_raw[b][:, g, :].rearrange("p (m t c) -> p t m c", t=4, c=2))
-            nc.vector.tensor_copy(out=w_scales[b, g][:].rearrange("p (t m) -> p t m", t=4),
-                                  in_=w_scale_raw[:, g, 512 * b:512 * b + 512].rearrange("p (m t) -> p t m", t=4))
+        def sort_l_codes(first, last):
+            raw = l_first[:] if first == 0 else l_rest[:, 1024 * (first - 1):1024 * (last - 1)]
+            sort_codes(l_codes[:, first:last, :], raw.rearrange("p (g n) -> p g n", n=1024))
+
+        def sort_l_scales(first, last):
+            sort_scales(l_scales[:, first:last, :],
+                        l_scale_raw[:, 512 * first:512 * last].rearrange("p (g n) -> p g n", n=512))
+
+        w_codes = {b: kept("w_codes%d" % b, [P, 4, 1024], U8) for b in (1, 2)}
+
+        def sort_w_codes(b, first, last):
+            sort_codes(w_codes[b][:, first:last, :], w_raw[b][:, first:last, :])
+
+        packed_sorted = kept("packed_sorted", [P, 1, 512], U8)
+
+        def sort_w_scales():
+            sort_scales(packed_sorted[:], packed[:])
+            for b in (2, 1):
+                for g in range(4):
+                    for q in range(4):
+                        row = 64 * (b - 1) + 16 * g + 4 * q
+                        nc.sync.dma_start(out=w_scales[b][32 * q:32 * q + 4, g, :].bitcast(I32),
+                                          in_=packed_sorted[row:row + 4, 0, :].bitcast(I32))
 
         growth, prices = {}, {}
         v_codes = {(h, g): kept("v_codes%d_%d" % (h, g), [P, 512], U32) for h in range(2) for g in range(4)}
@@ -154,7 +175,7 @@ def tile_guaranteed_basket_payoffs_h1_kernel(
 
         def exponentials(k, pairs=(0, 1)):
             h, g, q = place(k)
-            c = 2 * h + q
+            cols = slice(256 * q, 256 * q + 256)
             if pairs[0] == 0:
                 growth[k] = passing("growth", [P, 2, 256, 2], F32, LOOKAHEAD + 1)
             for u in pairs:
@@ -163,27 +184,25 @@ def tile_guaranteed_basket_payoffs_h1_kernel(
                     t = 2 * u + e
                     nc.tensor.matmul_mx(
                         out=x[:, 256 * e:256 * e + 256],
-                        lhsT=l_codes[g][:, 256 * t:256 * t + 256].bitcast(FP4X4),
-                        lhsT_scale=l_scales[g][:, P * t:P * t + P],
-                        rhs=z_codes[c][:].bitcast(FP8X4), rhs_scale=z_scales[c][:],
+                        lhsT=l_codes[:, g, 256 * t:256 * t + 256].bitcast(FP4X4),
+                        lhsT_scale=l_scales[:, g, P * t:P * t + P],
+                        rhs=z_codes[h][:, cols].bitcast(FP8X4), rhs_scale=z_scales[h][:, cols],
                         start=True, stop=True)
                 nc.scalar.activation(out=growth[k][:, u, :, :], in_=x[:].rearrange("p (e n) -> p n e", e=2),
                                      func=ACT.Exp)
 
         def times_median(k):
             h, g, q = place(k)
-            prices[k] = passing("prices", [P, 1024], BF16, 3)
+            if q == 0:
+                prices[h, g] = passing("prices", [P, 2048], BF16, 2)
             nc.vector.tensor_tensor(
-                out=prices[k][:].rearrange("p (n u e) -> p n u e", u=2, e=2),
+                out=prices[h, g][:, 1024 * q:1024 * q + 1024].rearrange("p (n u e) -> p n u e", u=2, e=2),
                 in0=growth[k][:].rearrange("p u n e -> p n u e"),
                 in1=median_sb[:, g, :].rearrange("p (u e) -> p u e", e=2).unsqueeze(1).to_broadcast([P, 256, 2, 2]),
                 op=ALU.mult)
 
-        def quantise_prices(k):
-            h, g, q = place(k)
-            cols = slice(256 * q, 256 * q + 256)
-            nc.vector.quantize_mx(out=v_codes[h, g][:, cols].bitcast(FP8X4), scales=v_scales[h, g][:, cols],
-                                  in_=prices[k][:])
+        def quantise_prices(h, g):
+            nc.vector.quantize_mx(out=v_codes[h, g][:].bitcast(FP8X4), scales=v_scales[h, g][:], in_=prices[h, g][:])
 
         natural = kept("natural", [P, 48], BF16)
 
@@ -206,8 +225,8 @@ def tile_guaranteed_basket_payoffs_h1_kernel(
                 codes = w_raw[b][:, g, 256 * t:256 * t + 256]
                 scales = w_scale_raw[:, g, 512 * b + P * t:512 * b + P * t + P]
             else:
-                codes = w_codes[b, g][:, 256 * t:256 * t + 256]
-                scales = w_scales[b, g][:, P * t:P * t + P]
+                codes = w_codes[b][:, g, 256 * t:256 * t + 256]
+                scales = w_scales[b][:, g, P * t:P * t + P]
             nc.tensor.matmul_mx(out=sums[b, h, t][:], lhsT=codes.bitcast(FP4X4), lhsT_scale=scales,
                                 rhs=v_codes[h, g][:].bitcast(FP8X4), rhs_scale=v_scales[h, g][:],
                                 start=(g == 0), stop=(g == 3))
@@ -315,21 +334,23 @@ def tile_guaranteed_basket_payoffs_h1_kernel(
             waiting.extend([(b, h, t, g) for b, t in open_tiles[h]])
 
         turn_z(0)(S)
-        sort_l(0)
-        quantise_z(0)
+        sort_l_scales(0, 1)
+        sort_l_codes(0, 1)
+        sort_l_scales(1, 2)
+        quantise_z(0, 0, 256)
         turn_z(1)(S)
         exponentials(0)
-        sort_l(1)
-        quantise_z(1)
+        sort_l_codes(1, 2)
+        quantise_z(0, 256, 512)
         exponentials(1)
-        sort_l(2)
+        sort_l_scales(2, 4)
+        sort_l_codes(2, 3)
         exponentials(2)
         times_median(0)
         exponentials(3)
         times_median(1)
-        quantise_prices(0)
-        sort_l(3)
-        quantise_prices(1)
+        sort_l_codes(3, 4)
+        quantise_prices(0, 0)
         empty = [turn_z(2), turn_z(3)]
         turn_rows()
         exponentials(4)
@@ -340,65 +361,62 @@ def tile_guaranteed_basket_payoffs_h1_kernel(
         passes(0, 0)
         for k in range(2, 8):
             times_median(k)
-            if k > 2:
-                quantise_prices(k - 1)
-            if k in (2, 3):
-                quantise_z(k)
+            if k == 4:
+                quantise_z(1, 0, 512)
+            if k == 3:
+                sort_w_scales()
+            if k in (4, 6):
+                quantise_prices(0, k // 2 - 1)
             for u in range(2):
                 exponentials(k + 4, (u,))
                 issue(2)
             if k in (4, 6):
                 passes(0, k // 2 - 1)
-        sort_w(2, 0)
-        quantise_prices(7)
+        quantise_prices(0, 3)
+        exponentials(12)
         passes(0, 3)
         issue(6)
-        for g in range(1, 4):
-            sort_w(2, g)
-        rings["short"], rings["sum"] = [0, 1, 2, 6, 7], [3, 4, 5]
+        sort_w_codes(2, 0, 2)
+        sort_w_codes(2, 2, 4)
+        rings["short"], rings["sum"] = [2, 6, 7, 0, 1], [3, 4, 5]
         whole_tile(1, 0, 1)
         floors(0, 0)
         whole_tile(1, 0, 2)
         times_median(8)
-        exponentials(12)
         whole_tile(1, 0, 3)
         times_median(9)
-        quantise_prices(8)
+        floors(1, 0)
+        regroup(0, 0)
         for step in turn_payoff(0, 0):
             step(S)
         whole_tile(2, 0, 0)
-        floors(1, 0)
-        regroup(0, 0)
-        quantise_prices(9)
+        quantise_prices(1, 0)
         exponentials(13)
         whole_tile(2, 0, 1)
         times_median(10)
         exponentials(14)
         whole_tile(2, 0, 2)
         times_median(11)
-        quantise_prices(10)
         for step in turn_payoff(1, 0):
             step(S)
         whole_tile(2, 0, 3)
-        quantise_prices(11)
         exponentials(15)
         times_median(12)
+        quantise_prices(1, 1)
         rings["short"], rings["sum"] = [1, 2, 7, 0], [4, 5, 6, 3]
         passes(1, 0)
         issue(4)
         times_median(13)
-        quantise_prices(12)
         times_median(14)
-        quantise_prices(13)
+        quantise_prices(1, 2)
         floors(2, 0)
         passes(1, 1)
         issue(4)
         round_payoff(2, 0, S, 128, (0, 128))
-        sort_w(1, 0)
+        sort_w_codes(1, 0, 1)
         times_median(15)
-        quantise_prices(14)
-        sort_w(1, 1)
-        quantise_prices(15)
+        sort_w_codes(1, 1, 2)
+        quantise_prices(1, 3)
         for step in turn_payoff(2, 0):
             step(S)
         passes(1, 2)
@@ -406,29 +424,31 @@ def tile_guaranteed_basket_payoffs_h1_kernel(
         passes(1, 3)
         issue(4)
         rings["short"], rings["sum"] = [7, 0, 1, 2, 3], [4, 5, 6]
-        sort_w(1, 2)
+        sort_w_codes(1, 2, 3)
         round_payoff(0, 0)
-        floors(0, 1)
-        regroup(0, 1)
+        floor_and_scale(0, 1, 0)
         quantise_payoff(0, 0)
+        floor_and_scale(0, 1, 1)
+        round_payoff(2, 0, V, 256, (256,))
+        floor_and_scale(0, 1, 2)
+        floor_and_scale(0, 1, 3)
+        regroup(0, 1)
         whole_tile(2, 1, 0)
         whole_tile(2, 1, 1)
-        round_payoff(2, 0, S, 128, (256,))
-        sort_w(1, 3)
+        sort_w_codes(1, 3, 4)
+        quantise_payoff(2, 0)
         round_payoff(1, 0)
         for step in turn_payoff(0, 1):
             step(S)
         floor_and_scale(2, 1, 0)
         floor_and_scale(2, 1, 1)
         quantise_payoff(1, 0)
+        store_scales(0)
         whole_tile(2, 1, 2)
         whole_tile(2, 1, 3)
-        round_payoff(2, 0, S, 128, (384,))
         floor_and_scale(2, 1, 2)
         floor_and_scale(2, 1, 3)
         whole_tile(1, 1, 0)
-        quantise_payoff(2, 0)
-        store_scales(0)
         round_payoff(2, 1)
         for step in turn_payoff(2, 1):
             step(S)
@@ -448,5 +468,5 @@ def tile_guaranteed_basket_payoffs_h1_kernel(
         last[1](S)
         quantise_payoff(1, 1)
         last[2](S)
-        last[3](V)
+        last[3](S)
         store_scales(1)

from contextlib import ExitStack
from functools import partial

import concourse.mybir as mybir
from concourse.masks import make_identity

PATHS, DRIVERS, ASSETS, BASKETS = 1024, 512, 2048, 1536
FLOPS = 2 * PATHS * DRIVERS * ASSETS + 2 * PATHS * ASSETS * BASKETS

F32 = mybir.dt.float32
BF16 = mybir.dt.bfloat16
I32 = mybir.dt.int32
U32 = mybir.dt.uint32
U8 = mybir.dt.uint8
FP8X4 = mybir.dt.float8_e4m3fn_x4
FP4X4 = mybir.dt.float4_e2m1fn_x4
ACT = mybir.ActivationFunctionType
ALU = mybir.AluOpType

P = 128
LOOKAHEAD = 5
NATURAL = ((0, 0), (1, 0), (0, 1))


def tile_guaranteed_basket_payoffs_h1_kernel(
    tc, z, loadings_words, loadings_scales, median, holdings_words, holdings_scales,
    cash, guarantee, notional, out_0, out_1, out_2,
):
    nc = tc.nc
    with ExitStack() as ctx:
        keep = ctx.enter_context(tc.tile_pool(name="keep", bufs=1))
        work = ctx.enter_context(tc.tile_pool(name="work", bufs=2))
        psum = ctx.enter_context(tc.psum_pool(name="psum", bufs=1))
        ctx.enter_context(tc.manual_schedule())

        def kept(name, shape, dtype):
            return keep.tile(shape, dtype, name=name, tag=name, align_bytes=64)

        def passing(name, shape, dtype, bufs):
            return work.tile(shape, dtype, name=name, tag=name, bufs=bufs, align_bytes=64)

        rings = {"short": [2, 3, 4, 5, 6, 7], "sum": []}

        def bank(kind, shape=None, dtype=F32):
            number = rings[kind][0]
            rings[kind] = rings[kind][1:] + [number]
            return psum.tile(shape or [P, 512], dtype, name="bank%d" % number, tag="bank%d" % number)

        l_scale_raw = kept("l_scale_raw", [P, ASSETS], U8)
        w_scale_raw = kept("w_scale_raw", [P, 4, 1024], U8)
        warm = kept("warm", [P, 2], F32)
        nc.vector.memset(l_scale_raw[:].bitcast(I32), 0)
        nc.vector.memset(warm[:], 0.0)
        nc.vector.memset(w_scale_raw[:].rearrange("p g n -> p (g n)").bitcast(I32), 0)
        median_sb = kept("median_sb", [P, 4, 4], BF16)
        nc.scalar.dma_start(out=median_sb[:], in_=median.rearrange("(g p t) -> p g t", p=P, t=4))
        nc.scalar.activation(out=warm[:, 1:2], in_=warm[:, 0:1], func=ACT.Exp)

        ident = kept("ident", [P, P], F32)
        make_identity(nc, ident[:])
        rows = kept("rows", [P, P], BF16)
        nc.gpsimd.memset(rows[:], 0.0)
        ident_bf = kept("ident_bf", [P, P], BF16)
        make_identity(nc, ident_bf[:])
        w_scales = {b: kept("w_scales%d" % b, [P, 4, 512], U8) for b in (1, 2)}
        for b in (2, 1):
            nc.gpsimd.memset(w_scales[b][:].rearrange("p g n -> p (g n)").bitcast(I32), 0)
        packed = kept("packed", [P, 1, 512], U8)
        slotted = [kept("slotted%d" % i, [P, 3, 4], BF16) for i in range(3)]

        z_raw = [kept("z_raw%d" % c, [P, 2, DRIVERS], BF16) for c in range(4)]
        l_first = kept("l_first", [P, 1024], U8)
        l_rest = kept("l_rest", [P, 3072], U8)
        w_raw = [kept("w_raw%d" % b, [P, 4, 1024], U8) for b in range(3)]

        def load_z(c):
            nc.sync.dma_start(out=z_raw[c][:], in_=z[256 * c:256 * c + 256, :].rearrange("(j p) k -> p j k", p=P))

        def load_w(b):
            nc.sync.dma_start(
                out=w_raw[b][:].bitcast(I32),
                in_=holdings_words[:, :, 1024 * b:1024 * b + 1024].rearrange("g p n -> p g n").bitcast(I32))

        load_z(0)
        for q in range(4):
            nc.sync.dma_start(out=l_scale_raw[32 * q:32 * q + 4, :].bitcast(I32),
                              in_=loadings_scales[0, 4 * q:4 * q + 4, :].bitcast(I32))
        nc.sync.dma_start(out=l_first[:].bitcast(I32), in_=loadings_words[0, :, 0:1024].bitcast(I32))
        load_z(1)
        nc.sync.dma_start(out=l_rest[:].bitcast(I32), in_=loadings_words[0, :, 1024:4096].bitcast(I32))
        for q in range(4):
            nc.sync.dma_start(out=w_scale_raw[32 * q:32 * q + 4, :, :].bitcast(I32),
                              in_=holdings_scales[:, 4 * q:4 * q + 4, 0:1024].rearrange("g r n -> r g n").bitcast(I32))
        load_z(2)
        load_z(3)
        for i, vec in enumerate((cash, guarantee, notional)):
            nc.sync.dma_start(out=rows[16 * i:16 * i + 12, :], in_=vec.rearrange("(j p) -> j p", p=P))
        load_w(0)
        for b in (1, 2):
            nc.sync.dma_start(
                out=packed[64 * (b - 1):64 * b, 0, :].bitcast(I32),
                in_=holdings_scales[:, :, 512 * b:512 * b + 512].rearrange("g q n -> (g q) n").bitcast(I32))
        load_w(1)
        load_w(2)
        for i, vec in enumerate((cash, guarantee, notional)):
            nc.sync.dma_start(out=slotted[i][:], in_=vec.rearrange("(b p t) -> p b t", p=P, t=4))

        def copy_on(engine, out, in_):
            if engine == "scalar":
                nc.scalar.copy(out=out, in_=in_)
            else:
                nc.vector.tensor_copy(out=out, in_=in_)

        def turn_words(sources, grouped):
            turned = bank("short")
            for i, source in enumerate(sources):
                nc.tensor.transpose(turned[:, P * i:P * i + P], source, ident[:])
            return lambda engine: copy_on(engine, grouped.rearrange("p (j r u) -> p j r u", j=2, u=2),
                                          turned[:].rearrange("p (j u r) -> p j r u", j=2, u=2))

        z_grouped = [kept("z_grouped%d" % h, [P, 1024], F32) for h in range(2)]
        z_codes = [kept("z_codes%d" % h, [P, 512], U32) for h in range(2)]
        z_scales = [kept("z_scales%d" % h, [P, 512], U8) for h in range(2)]

        def turn_z(c):
            words = z_raw[c][:].rearrange("p j k -> p (j k)").bitcast(F32)
            return turn_words([words[:, 256 * j + u:256 * j + 256:2] for j in range(2) for u in range(2)],
                              z_grouped[c // 2][:, 512 * (c % 2):512 * (c % 2) + 512])

        def quantise_z(h, first, last):
            nc.vector.quantize_mx(out=z_codes[h][:, first:last].bitcast(FP8X4), scales=z_scales[h][:, first:last],
                                  in_=z_grouped[h][:, 2 * first:2 * last].bitcast(BF16))

        def sort_codes(target, raw):
            nc.vector.tensor_copy(out=target.rearrange("p g (t m c) -> p g t m c", t=4, c=2),
                                  in_=raw.rearrange("p g (m t c) -> p g t m c", t=4, c=2))

        def sort_scales(target, raw):
            nc.vector.tensor_copy(out=target.rearrange("p g (t m) -> p g t m", t=4),
                                  in_=raw.rearrange("p g (m t) -> p g t m", t=4))

        l_codes = kept("l_codes", [P, 4, 1024], U8)
        l_scales = kept("l_scales", [P, 4, 512], U8)

        def sort_l_codes(first, last):
            raw = l_first[:] if first == 0 else l_rest[:, 1024 * (first - 1):1024 * (last - 1)]
            sort_codes(l_codes[:, first:last, :], raw.rearrange("p (g n) -> p g n", n=1024))

        def sort_l_scales(first, last):
            sort_scales(l_scales[:, first:last, :],
                        l_scale_raw[:, 512 * first:512 * last].rearrange("p (g n) -> p g n", n=512))

        w_codes = {b: kept("w_codes%d" % b, [P, 4, 1024], U8) for b in (1, 2)}

        def sort_w_codes(b, first, last):
            sort_codes(w_codes[b][:, first:last, :], w_raw[b][:, first:last, :])

        packed_sorted = kept("packed_sorted", [P, 1, 512], U8)

        def sort_w_scales():
            sort_scales(packed_sorted[:], packed[:])
            for b in (2, 1):
                for g in range(4):
                    for q in range(4):
                        row = 64 * (b - 1) + 16 * g + 4 * q
                        nc.sync.dma_start(out=w_scales[b][32 * q:32 * q + 4, g, :].bitcast(I32),
                                          in_=packed_sorted[row:row + 4, 0, :].bitcast(I32))

        growth, prices = {}, {}
        v_codes = {(h, g): kept("v_codes%d_%d" % (h, g), [P, 512], U32) for h in range(2) for g in range(4)}
        v_scales = {(h, g): kept("v_scales%d_%d" % (h, g), [P, 512], U8) for h in range(2) for g in range(4)}

        def place(k):
            return k // 8, (k % 8) // 2, k % 2

        def exponentials(k, pairs=(0, 1)):
            h, g, q = place(k)
            cols = slice(256 * q, 256 * q + 256)
            if pairs[0] == 0:
                growth[k] = passing("growth", [P, 2, 256, 2], F32, LOOKAHEAD + 1)
            for u in pairs:
                x = bank("short")
                for e in range(2):
                    t = 2 * u + e
                    nc.tensor.matmul_mx(
                        out=x[:, 256 * e:256 * e + 256],
                        lhsT=l_codes[:, g, 256 * t:256 * t + 256].bitcast(FP4X4),
                        lhsT_scale=l_scales[:, g, P * t:P * t + P],
                        rhs=z_codes[h][:, cols].bitcast(FP8X4), rhs_scale=z_scales[h][:, cols],
                        start=True, stop=True)
                nc.scalar.activation(out=growth[k][:, u, :, :], in_=x[:].rearrange("p (e n) -> p n e", e=2),
                                     func=ACT.Exp)

        def times_median(k):
            h, g, q = place(k)
            if q == 0:
                prices[h, g] = passing("prices", [P, 2048], BF16, 2)
            nc.vector.tensor_tensor(
                out=prices[h, g][:, 1024 * q:1024 * q + 1024].rearrange("p (n u e) -> p n u e", u=2, e=2),
                in0=growth[k][:].rearrange("p u n e -> p n u e"),
                in1=median_sb[:, g, :].rearrange("p (u e) -> p u e", e=2).unsqueeze(1).to_broadcast([P, 256, 2, 2]),
                op=ALU.mult)

        def quantise_prices(h, g):
            nc.vector.quantize_mx(out=v_codes[h, g][:].bitcast(FP8X4), scales=v_scales[h, g][:], in_=prices[h, g][:])

        natural = kept("natural", [P, 48], BF16)

        def turn_rows():
            turned = bank("short", [P, P], BF16)
            nc.tensor.transpose(turned[:], rows[:], ident_bf[:])
            nc.scalar.copy(out=natural[:], in_=turned[:, 0:48])

        def column(i, b, h, t):
            if (b, h) in NATURAL:
                return natural[:, 16 * i + 4 * b + t:16 * i + 4 * b + t + 1]
            return slotted[i][:, b, t:t + 1]

        sums, payoff, pair, regrouped = {}, {}, [], {}

        def one_pass(b, h, t, g):
            if g == 0:
                sums[b, h, t] = bank("sum")
            if (b, h) in NATURAL:
                codes = w_raw[b][:, g, 256 * t:256 * t + 256]
                scales = w_scale_raw[:, g, 512 * b + P * t:512 * b + P * t + P]
            else:
                codes = w_codes[b][:, g, 256 * t:256 * t + 256]
                scales = w_scales[b][:, g, P * t:P * t + P]
            nc.tensor.matmul_mx(out=sums[b, h, t][:], lhsT=codes.bitcast(FP4X4), lhsT_scale=scales,
                                rhs=v_codes[h, g][:].bitcast(FP8X4), rhs_scale=v_scales[h, g][:],
                                start=(g == 0), stop=(g == 3))

        def add_cash(b, h, t):
            if (b, h) == (0, 0) and t == 0:
                both = kept("both", [P, 4, 2, 512], F32)
                pair.append(both)
                payoff[0, 0], payoff[1, 0] = both[:, :, 0, :], both[:, :, 1, :]
            elif t == 0 and (b, h) != (1, 0):
                payoff[b, h] = passing("payoff", [P, 4, 512], F32, 5)[:]
            nc.scalar.activation(out=payoff[b, h][:, t, :], in_=sums[b, h, t][:], func=ACT.Identity,
                                 bias=column(0, b, h, t))

        def whole_tile(b, h, t):
            for g in range(4):
                one_pass(b, h, t, g)
            add_cash(b, h, t)

        def floor_and_scale(b, h, t):
            nc.vector.tensor_scalar(out=payoff[b, h][:, t, :], in0=payoff[b, h][:, t, :],
                                    scalar1=column(1, b, h, t), scalar2=column(2, b, h, t), op0=ALU.max, op1=ALU.mult)

        by_path = {}

        def store_paths(b, h, j0, j1):
            nc.sync.dma_start(
                out=out_0[512 * h + P * j0:512 * h + P * j1, 512 * b:512 * b + 512].rearrange("(j p) n -> p j n", p=P),
                in_=by_path[b, h][:, j0:j1, :])

        def empty_block(b, h, j, turned, engine, stored):
            if (b, h) in NATURAL:
                copy_on(engine, by_path[b, h][:, j, :], turned[:])
            else:
                copy_on(engine, by_path[b, h][:, j, :].rearrange("p (m t) -> p m t", t=4),
                        turned[:].rearrange("p (t m) -> p m t", t=4))
            if (j + 1) % stored == 0:
                store_paths(b, h, j + 1 - stored, j + 1)

        def turn_payoff(b, h, stored=2, blocks=(0, 1, 2, 3)):
            if blocks[0] == 0:
                by_path[b, h] = passing("by_path", [P, 4, 512], F32, 3)
            turned = {j: bank("short") for j in blocks}
            for t in range(4):
                for j in blocks:
                    nc.tensor.transpose(turned[j][:, P * t:P * t + P], payoff[b, h][:, t, P * j:P * j + P], ident[:])
            return [partial(empty_block, b, h, j, turned[j], stored=stored) for j in blocks]

        y_grouped, y_sorted = {}, {}
        y_scales = [kept("y_scales%d" % h, [P, 3, 512], U8) for h in range(2)]

        def regroup(b, h):
            if (b, h) == (0, 0):
                source = pair[0][:]
                target = kept("regrouped", [P, 4, 2, 512], F32)[:]
                regrouped[0, 0], regrouped[1, 0] = target[:, :, 0, :], target[:, :, 1, :]
            else:
                source = payoff[b, h].unsqueeze(2)
                regrouped[b, h] = passing("payoff", [P, 4, 512], F32, 5)[:]
                target = regrouped[b, h].unsqueeze(2)
            for j in range(4):
                for t in range(4):
                    nc.sync.dma_start(out=target[32 * j:32 * j + 32, t, :, :], in_=source[t:P:4, j, :, :])

        def round_payoff(b, h, engine="vector", width=512, starts=(0,)):
            source = regrouped[b, h] if (b, h) in NATURAL else payoff[b, h]
            if starts[0] == 0:
                y_grouped[b, h] = passing("y_grouped", [P, 2048], BF16, 3)
            for a in starts:
                copy_on(engine,
                        y_grouped[b, h][:, 4 * a:4 * a + 4 * width].rearrange("p (c i t) -> p c t i", i=2, t=4),
                        source[:, :, a:a + width].rearrange("p t (c i) -> p c t i", i=2))

        def quantise_payoff(b, h):
            codes = passing("y_codes", [P, 512], U32, 3)
            cols = slice(512 * h, 512 * h + 512)
            nc.vector.quantize_mx(out=codes[:].bitcast(FP8X4), scales=y_scales[h][:, b, :],
                                  in_=y_grouped[b, h][:])
            nc.sync.dma_start(out=out_1[b, :, cols, :].rearrange("p m t -> p (m t)").bitcast(I32),
                              in_=codes[:].bitcast(I32))

        def store_scales(h):
            for q in range(4):
                nc.sync.dma_start(
                    out=out_2[:, 4 * q:4 * q + 4, 512 * h:512 * h + 512].rearrange("b r m -> r b m").bitcast(I32),
                    in_=y_scales[h][32 * q:32 * q + 4, :, :].bitcast(I32))

        S, V = "scalar", "vector"
        open_tiles = {0: [(0, 0), (0, 1), (0, 2), (0, 3), (1, 0)], 1: [(0, 0), (0, 1), (0, 2), (0, 3)]}
        waiting = []

        def issue(count):
            for i in range(min(count, len(waiting))):
                b, h, t, g = waiting[0]
                waiting.remove(waiting[0])
                one_pass(b, h, t, g)
                if g == 3:
                    add_cash(b, h, t)

        def floors(b, h):
            for t in range(4):
                floor_and_scale(b, h, t)

        def passes(h, g):
            waiting.extend([(b, h, t, g) for b, t in open_tiles[h]])

        turn_z(0)(S)
        sort_l_scales(0, 1)
        sort_l_codes(0, 1)
        sort_l_scales(1, 2)
        quantise_z(0, 0, 256)
        turn_z(1)(S)
        exponentials(0)
        sort_l_codes(1, 2)
        quantise_z(0, 256, 512)
        exponentials(1)
        sort_l_scales(2, 4)
        sort_l_codes(2, 3)
        exponentials(2)
        times_median(0)
        exponentials(3)
        times_median(1)
        sort_l_codes(3, 4)
        quantise_prices(0, 0)
        empty = [turn_z(2), turn_z(3)]
        turn_rows()
        exponentials(4)
        empty[0](S)
        exponentials(5)
        empty[1](S)
        rings["short"], rings["sum"] = [0, 1, 2], [3, 4, 5, 6, 7]
        passes(0, 0)
        for k in range(2, 8):
            times_median(k)
            if k == 4:
                quantise_z(1, 0, 512)
            if k == 3:
                sort_w_scales()
            if k in (4, 6):
                quantise_prices(0, k // 2 - 1)
            for u in range(2):
                exponentials(k + 4, (u,))
                issue(2)
            if k in (4, 6):
                passes(0, k // 2 - 1)
        quantise_prices(0, 3)
        exponentials(12)
        passes(0, 3)
        issue(6)
        sort_w_codes(2, 0, 2)
        sort_w_codes(2, 2, 4)
        rings["short"], rings["sum"] = [2, 6, 7, 0, 1], [3, 4, 5]
        whole_tile(1, 0, 1)
        floors(0, 0)
        whole_tile(1, 0, 2)
        times_median(8)
        whole_tile(1, 0, 3)
        times_median(9)
        floors(1, 0)
        regroup(0, 0)
        for step in turn_payoff(0, 0):
            step(S)
        whole_tile(2, 0, 0)
        quantise_prices(1, 0)
        exponentials(13)
        whole_tile(2, 0, 1)
        times_median(10)
        exponentials(14)
        whole_tile(2, 0, 2)
        times_median(11)
        for step in turn_payoff(1, 0):
            step(S)
        whole_tile(2, 0, 3)
        exponentials(15)
        times_median(12)
        quantise_prices(1, 1)
        rings["short"], rings["sum"] = [1, 2, 7, 0], [4, 5, 6, 3]
        passes(1, 0)
        issue(4)
        times_median(13)
        times_median(14)
        quantise_prices(1, 2)
        floors(2, 0)
        passes(1, 1)
        issue(4)
        round_payoff(2, 0, S, 128, (0, 128))
        sort_w_codes(1, 0, 1)
        times_median(15)
        sort_w_codes(1, 1, 2)
        quantise_prices(1, 3)
        for step in turn_payoff(2, 0):
            step(S)
        passes(1, 2)
        issue(4)
        passes(1, 3)
        issue(4)
        rings["short"], rings["sum"] = [7, 0, 1, 2, 3], [4, 5, 6]
        sort_w_codes(1, 2, 3)
        round_payoff(0, 0)
        floor_and_scale(0, 1, 0)
        quantise_payoff(0, 0)
        floor_and_scale(0, 1, 1)
        round_payoff(2, 0, V, 256, (256,))
        floor_and_scale(0, 1, 2)
        floor_and_scale(0, 1, 3)
        regroup(0, 1)
        whole_tile(2, 1, 0)
        whole_tile(2, 1, 1)
        sort_w_codes(1, 3, 4)
        quantise_payoff(2, 0)
        round_payoff(1, 0)
        for step in turn_payoff(0, 1):
            step(S)
        floor_and_scale(2, 1, 0)
        floor_and_scale(2, 1, 1)
        quantise_payoff(1, 0)
        store_scales(0)
        whole_tile(2, 1, 2)
        whole_tile(2, 1, 3)
        floor_and_scale(2, 1, 2)
        floor_and_scale(2, 1, 3)
        whole_tile(1, 1, 0)
        round_payoff(2, 1)
        for step in turn_payoff(2, 1):
            step(S)
        floor_and_scale(1, 1, 0)
        quantise_payoff(2, 1)
        whole_tile(1, 1, 1)
        round_payoff(0, 1)
        whole_tile(1, 1, 2)
        floor_and_scale(1, 1, 1)
        quantise_payoff(0, 1)
        floor_and_scale(1, 1, 2)
        whole_tile(1, 1, 3)
        floor_and_scale(1, 1, 3)
        round_payoff(1, 1)
        last = turn_payoff(1, 1, stored=1)
        last[0](S)
        last[1](S)
        quantise_payoff(1, 1)
        last[2](S)
        last[3](S)
        store_scales(1)
